import numpy as np
import ml_dtypes


def mxq(x, axis, fmt="e4m3"):
    dtype, down = {"e4m3": (ml_dtypes.float8_e4m3fn, 7), "e5m2": (ml_dtypes.float8_e5m2, 14)}[fmt]
    v = np.moveaxis(np.asarray(x, np.float32).astype(ml_dtypes.bfloat16).astype(np.float64), axis, -1)
    blocks = v.reshape(v.shape[:-1] + (-1, 32))
    amax = np.abs(blocks).max(-1, keepdims=True)
    byte = np.maximum(np.where(amax > 0, np.frexp(amax)[1] - 1 + 127, 0) - down, 1)
    scale = np.exp2(byte - 127.0)
    codes = (blocks / scale).astype(np.float32).astype(dtype).astype(np.float64)
    return np.moveaxis((codes * scale).reshape(v.shape), -1, axis)


WIDE = False


def mx_kscale(k):
    if not WIDE:
        return np.ones(k)
    levels = np.array([10, -10, 5, -5, 0])
    if k % 512:
        return np.exp2(np.random.permutation(np.resize(levels, k // 32))).repeat(32)
    a = np.empty((k // 512, 16))
    for p in range(k // 512):
        a[p, :8] = np.random.permutation(np.resize(levels, 8))
        for g in range(8):
            far = levels[np.abs(levels - a[p, g]) >= 10]
            a[p, g + 8] = far[np.random.randint(len(far))]
    return np.exp2(a.ravel()).repeat(32)


def f64(x):
    return np.asarray(x).astype(np.float64)


def striped(idx):
    return np.tile(idx.reshape(-1, 16).T, (8, 1)).astype(np.uint16)


def unstriped(offs):
    return offs[:16].T.reshape(-1).astype(np.int64)


E2M1 = np.array([0.0, 0.5, 1.0, 1.5, 2.0, 3.0, 4.0, 6.0, -0.0, -0.5, -1.0, -1.5, -2.0, -3.0, -4.0, -6.0])


def pack_weight(w, fmt):
    k, n = w.shape
    w = f64(np.asarray(w, np.float32).astype(ml_dtypes.bfloat16)).reshape(k // 32, 32, n)
    amax = np.abs(w).max(1)
    if fmt == "e4m3":
        byte = np.frexp(amax)[1] - 1 + 127 - 7
    else:
        mant, ex = np.frexp(amax / 6.0)
        byte = np.where(mant > 0.5, ex, ex - 1) + 127
    byte = np.clip(np.where(amax > 0, byte, 1), 1, 254)
    scaled = (w * np.exp2(127.0 - byte)[:, None, :]).reshape(k, n).astype(np.float32)
    by_word = np.ascontiguousarray(scaled.reshape(k // 512, 128, 4, n).transpose(0, 1, 3, 2))
    if fmt == "e4m3":
        words = by_word.astype(ml_dtypes.float8_e4m3fn).view(np.uint8)
    else:
        c = by_word.astype(ml_dtypes.float4_e2m1fn).view(np.uint8) & 0xF
        words = (c[..., 0::2] | (c[..., 1::2] << 4)).reshape(k // 512, 128, 2 * n)
    return np.ascontiguousarray(words), np.ascontiguousarray(byte.astype(np.uint8).reshape(k // 512, 16, n))


def unpack_weight(words, scales, fmt):
    g, _, n = scales.shape
    words = np.ascontiguousarray(words).reshape(g, 128, n, -1)
    if fmt == "e4m3":
        vals = words.view(ml_dtypes.float8_e4m3fn).astype(np.float64)
    else:
        nib = np.empty((g, 128, n, 4), np.uint8)
        nib[..., 0::2] = words & 0xF
        nib[..., 1::2] = words >> 4
        vals = E2M1[nib]
    vals = vals * np.repeat(np.exp2(scales.astype(np.float64) - 127.0), 8, axis=1)[..., None]
    return vals.transpose(0, 1, 3, 2).reshape(g * 512, n)


def pack_table4(v):
    words, scales = pack_weight(v, "e2m1")
    g, t = words.shape[0] // 2, v.shape[1]
    words = words.reshape(g, 2, 128, t, 2).transpose(0, 2, 3, 1, 4)
    return np.concatenate([words.reshape(g, -1), scales.reshape(g, -1)], axis=1)


def unpack_table4(tab):
    g, t = tab.shape[0], tab.shape[1] // 544
    words = tab[:, :512 * t].reshape(g, 128, t, 2, 2).transpose(0, 3, 1, 2, 4).reshape(2 * g, 128, 2 * t)
    return unpack_weight(words, tab[:, 512 * t:].reshape(2 * g, 16, t), "e2m1")


def gelu(v):
    return 0.5 * v * (1.0 + np.tanh(np.sqrt(2.0 / np.pi) * (v + 0.044715 * v**3)))


K, M, T, S = 1024, 1024, 4096, 2048


def setup_inputs():
    n = np.random.standard_normal
    s = mx_kscale(K)[:, None]
    return {
        "tab": pack_table4(n((K, T)) * s),
        "w": (n((K, M)) / np.sqrt(K) / s).astype(np.float32),
        "b": (0.3 * n(1024)).astype(np.float32),
        "offs": striped(np.random.permutation(T)[:S]),
    }


def reference(tab, w, b, offs):
    tab_ = unpack_table4(tab)[:, unstriped(offs)]
    w_ = mxq(f64(w), 0, "e4m3")
    y = w_.T @ tab_
    return gelu(y + f64(b)[:, None])

@@ -1,0 +1,204 @@
+from contextlib import ExitStack
+
+import concourse.mybir as mybir
+
+K, M, T, S = 1024, 1024, 4096, 2048
+FLOPS = 2 * K * M * S
+
+F32 = mybir.dt.float32
+BF16 = mybir.dt.bfloat16
+I32 = mybir.dt.int32
+U32 = mybir.dt.uint32
+U16 = mybir.dt.uint16
+U8 = mybir.dt.uint8
+E4M3 = mybir.dt.float8_e4m3fn_x4
+E2M1 = mybir.dt.float4_e2m1fn_x4
+GELU = mybir.ActivationFunctionType.Gelu_apprx_tanh
+
+P = 128
+PASSES = 2
+N = 512
+SLICES = S // N
+HALF = 512
+M_TILES = M // P
+
+
+def tile_list_tab4_gelu_kernel(tc, tab, w, b, offs, out):
+    nc = tc.nc
+    with ExitStack() as ctx:
+        keep = ctx.enter_context(tc.tile_pool(name="keep", bufs=1))
+        psum = ctx.enter_context(tc.psum_pool(name="psum", bufs=8))
+
+        offsets = keep.tile([P, S // 16], U16, name="offsets")
+        words = keep.tile([P, T], I32, name="words")
+        planes = keep.tile([P, PASSES, T], U8, name="planes", align_bytes=64)
+        b_rows = keep.tile([P, 32], F32, name="b_rows", align_bytes=64)
+        b_cols = keep.tile([P, 32], F32, name="b_cols", align_bytes=64)
+        warm = keep.tile([P, 1], F32, name="warm")
+
+        nc.sync.dma_start(offsets[:], offs)
+        nc.vector.memset(planes[:, 0, :].bitcast(I32), 0)
+        nc.gpsimd.memset(planes[:, 1, :].bitcast(I32), 0)
+        nc.vector.memset(words[:, 0:1], 0)
+        nc.gpsimd.memset(b_rows[:], 0.0)
+        nc.vector.memset(warm[:], 0.0)
+        nc.scalar.activation(warm[:], warm[:], GELU)
+
+        scale_rows = tab[0, 512 * T : 544 * T].rearrange("(h q t) -> q h t", h=PASSES, t=T)
+        for q in range(4):
+            nc.sync.dma_start(
+                out=planes[32 * q : 32 * q + 4, :, :].bitcast(I32),
+                in_=scale_rows[4 * q : 4 * q + 4, :, :].bitcast(I32),
+            )
+        nc.sync.dma_start(
+            out=words[:],
+            in_=tab[0, 0 : 512 * T].rearrange("(p c) -> p c", p=P).bitcast(I32),
+        )
+        b_view = b.rearrange("(j q r) -> q j r", q=4, r=32)
+        for q in range(4):
+            nc.scalar.dma_start(out=b_rows[32 * q : 32 * q + M_TILES, :], in_=b_view[q])
+
+        chunks = [(0, 256), (256, 256), (512, 512)]
+        w_raw = {}
+        for k, (c0, width) in enumerate(chunks):
+            for a in range(PASSES):
+                raw = keep.tile([P, 4, width], F32, name=f"raw{k}{a}")
+                nc.vector.memset(raw[:, 0, 0:1], 0.0)
+                nc.sync.dma_start(
+                    out=raw[:],
+                    in_=w[512 * a : 512 * a + 512, c0 : c0 + width].rearrange("(p i) c -> p i c", i=4),
+                )
+                w_raw[k, a] = raw
+        nc.vector.transpose(b_cols[:], b_rows[:])
+
+        g_words, g_scales, parted = {}, {}, {}
+        w_codes = keep.tile([P, PASSES, M], U32, name="w_codes", align_bytes=64)
+        w_scales = keep.tile([P, PASSES, M], U8, name="w_scales", align_bytes=64)
+        outs = {}
+        for m in range(M_TILES):
+            outs[m] = keep.tile([P, S], F32, name=f"outs{m}")
+
+        def list_of(s):
+            return offsets[:, s * (N // 16) : (s + 1) * (N // 16)]
+
+        scale_tags = {0: "sc0", 1: "sc1", 2: "turn01a", 3: "turn21a"}
+        word_tags = {0: "gw0", 1: "turn01b", 2: "turn11", 3: "turn21b"}
+
+        def gather_scales(s):
+            g = keep.tile([P, PASSES, N], U8, name=f"g_scales{s}", tag=scale_tags[s], align_bytes=64)
+            for h in range(PASSES):
+                nc.vector.tensor_copy(g[:, h, :], planes[:, h, :].indirect(list_of(s)))
+            g_scales[s] = g
+
+        def gather_words(s):
+            g = keep.tile([P, N], I32, name=f"g_words{s}", tag=word_tags[s], align_bytes=64)
+            nc.vector.tensor_copy(g[:].bitcast(U32), words[:].bitcast(U32).indirect(list_of(s)))
+            g_words[s] = g
+
+        def part(s):
+            t = keep.tile([P, PASSES, 2 * N], U8, name=f"parted{s}", align_bytes=64)
+            nc.vector.tensor_copy(
+                t[:].rearrange("p h c -> p (h c)").bitcast(U16).rearrange("p (h n) -> p h n", h=PASSES),
+                g_words[s][:].bitcast(U16).rearrange("p (n h) -> p h n", h=PASSES),
+            )
+            parted[s] = t
+
+        grouped = {}
+
+        def group(engine, k, a, c0, c1, tag):
+            t = keep.tile([P, c1 - c0, 4], BF16, name=f"grouped{k}{a}{c0}", tag=tag, align_bytes=64)
+            src = w_raw[k, a][:, :, c0:c1].rearrange("p i c -> p c i")
+            if engine == "scalar":
+                nc.scalar.copy(t[:], src)
+            elif engine == "gpsimd":
+                nc.gpsimd.tensor_copy(t[:], src)
+            else:
+                nc.vector.tensor_copy(t[:], src)
+            grouped[k, a, c0] = t
+
+        def quantize(k, a, c0, c1):
+            cols = slice(chunks[k][0] + c0, chunks[k][0] + c1)
+            nc.vector.quantize_mx(
+                out=w_codes[:, a, cols].bitcast(E4M3),
+                scales=w_scales[:, a, cols],
+                in_=grouped[k, a, c0][:].rearrange("p c i -> p (c i)"),
+            )
+
+        def product(m, s, step=N):
+            acc = psum.tile([P, N], F32, name="acc")
+            for a in range(PASSES):
+                nc.tensor.matmul_mx(
+                    out=acc[:],
+                    lhsT=w_codes[:, a, P * m : P * m + P].bitcast(E4M3),
+                    lhsT_scale=w_scales[:, a, P * m : P * m + P],
+                    rhs=parted[s][:, a, :].bitcast(E2M1),
+                    rhs_scale=g_scales[s][:, a, :],
+                    start=(a == 0),
+                    stop=(a == PASSES - 1),
+                )
+            for c in range(0, N, step):
+                nc.scalar.activation(
+                    outs[m][:, N * s + c : N * s + c + step], acc[:, c : c + step], GELU, bias=b_cols[:, m : m + 1]
+                )
+
+        def store(m, c0, c1):
+            nc.sync.dma_start(out=out[P * m : P * m + P, c0:c1], in_=outs[m][:, c0:c1])
+
+        gather_scales(0)
+        group("scalar", 0, 0, 0, 256, "turn00")
+        group("scalar", 0, 1, 0, 128, "turn01a")
+        group("gpsimd", 0, 1, 128, 256, "turn01b")
+        group("gpsimd", 1, 0, 0, 256, "turn10")
+        group("gpsimd", 1, 1, 0, 256, "turn11")
+        group("gpsimd", 2, 0, 0, 256, "turn20a")
+        group("gpsimd", 2, 0, 256, 512, "turn20b")
+        group("gpsimd", 2, 1, 256, 512, "turn21b")
+        gather_words(0)
+        part(0)
+        quantize(0, 0, 0, 256)
+        quantize(0, 1, 0, 128)
+        quantize(0, 1, 128, 256)
+        for m in range(2):
+            product(m, 0)
+        gather_scales(1)
+        gather_words(1)
+        part(1)
+        for m in range(2):
+            product(m, 1)
+            store(m, 0, 1024)
+        quantize(1, 0, 0, 256)
+        quantize(1, 1, 0, 256)
+        for m in range(2, 4):
+            product(m, 0)
+            product(m, 1)
+            store(m, 0, 1024)
+        gather_scales(2)
+        gather_words(2)
+        part(2)
+        for m in range(4):
+            product(m, 2)
+        group("vector", 2, 1, 0, 256, "turn21a")
+        quantize(2, 0, 0, 256)
+        quantize(2, 1, 0, 256)
+        quantize(2, 0, 256, 512)
+        quantize(2, 1, 256, 512)
+        for m in range(4, 8):
+            product(m, 0)
+            product(m, 1)
+            store(m, 0, 1024)
+        gather_scales(3)
+        gather_words(3)
+        part(3)
+        for m in range(4):
+            product(m, 3)
+            store(m, 1024, 2048)
+        for m in range(4, 8):
+            product(m, 2)
+            if m < 7:
+                product(m, 3)
+                store(m, 1024, 2048)
+            else:
+                store(m, 1024, 1536)
+                product(m, 3, step=256)
+                store(m, 1536, 1792)
+                store(m, 1792, 2048)

@@ -1,6 +1,7 @@
 from contextlib import ExitStack
 
 import concourse.mybir as mybir
+from concourse.masks import make_identity
 
 K, M, T, S = 1024, 1024, 4096, 2048
 FLOPS = 2 * K * M * S
@@ -21,6 +22,8 @@ N = 512
 SLICES = S // N
 HALF = 512
 M_TILES = M // P
+SHIFT = 16
+N_SCALES = 1024
 
 
 def tile_list_tab4_gelu_kernel(tc, tab, w, b, offs, out):
@@ -31,108 +34,107 @@ def tile_list_tab4_gelu_kernel(tc, tab, w, b, offs, out):
 
         offsets = keep.tile([P, S // 16], U16, name="offsets")
         words = keep.tile([P, T], I32, name="words")
-        planes = keep.tile([P, PASSES, T], U8, name="planes", align_bytes=64)
-        b_rows = keep.tile([P, 32], F32, name="b_rows", align_bytes=64)
-        b_cols = keep.tile([P, 32], F32, name="b_cols", align_bytes=64)
+        plane = keep.tile([P, T], U8, name="plane", tag="plane", align_bytes=64)
+        b_rows = keep.tile([P, P], F32, name="b_rows")
+        b_cols = keep.tile([P, M_TILES], F32, name="b_cols")
+        identity = keep.tile([P, P], F32, name="identity")
         warm = keep.tile([P, 1], F32, name="warm")
+        first = [keep.tile([P, N_SCALES], U8, name=f"first{i}", align_bytes=64) for i in range(2)]
+        second = [keep.tile([P, N_SCALES], U8, name=f"second{i}", align_bytes=64) for i in range(2)]
+        raws = {}
+        for a in range(PASSES):
+            raws[0, a] = keep.tile([P, 4, HALF], F32, name=f"raw{a}")[:]
+
+        def load_w(half, a):
+            nc.sync.dma_start(
+                out=raws[half, a],
+                in_=w[512 * a : 512 * a + 512, HALF * half : HALF * half + HALF].rearrange("(p i) c -> p i c", i=4),
+            )
 
         nc.sync.dma_start(offsets[:], offs)
-        nc.vector.memset(planes[:, 0, :].bitcast(I32), 0)
-        nc.gpsimd.memset(planes[:, 1, :].bitcast(I32), 0)
+        load_w(0, 0)
+
+        nc.vector.memset(plane[:].bitcast(I32), 0)
         nc.vector.memset(words[:, 0:1], 0)
-        nc.gpsimd.memset(b_rows[:], 0.0)
+        nc.vector.memset(raws[0, 1][:, 0, 0:1], 0.0)
         nc.vector.memset(warm[:], 0.0)
+        nc.gpsimd.memset(b_rows[:], 0.0)
+        make_identity(nc, identity[:])
+        for i in range(2):
+            nc.gpsimd.memset(second[i][:].bitcast(I32), 0)
+        nc.scalar.dma_start(out=b_rows[0:M_TILES, :], in_=b.rearrange("(j p) -> j p", p=P))
         nc.scalar.activation(warm[:], warm[:], GELU)
 
-        scale_rows = tab[0, 512 * T : 544 * T].rearrange("(h q t) -> q h t", h=PASSES, t=T)
-        for q in range(4):
-            nc.sync.dma_start(
-                out=planes[32 * q : 32 * q + 4, :, :].bitcast(I32),
-                in_=scale_rows[4 * q : 4 * q + 4, :, :].bitcast(I32),
-            )
+        scale_rows = tab[0, 512 * T : 544 * T].rearrange("(q t) -> q t", t=T)
+        for h in range(PASSES):
+            queue = nc.sync if h == 0 else nc.gpsimd
+            for q in range(4):
+                p0 = 32 * q + SHIFT * h
+                queue.dma_start(
+                    out=plane[p0 : p0 + 4, :].bitcast(I32),
+                    in_=scale_rows[16 * h + 4 * q : 16 * h + 4 * q + 4, :].bitcast(I32),
+                )
         nc.sync.dma_start(
             out=words[:],
             in_=tab[0, 0 : 512 * T].rearrange("(p c) -> p c", p=P).bitcast(I32),
         )
-        b_view = b.rearrange("(j q r) -> q j r", q=4, r=32)
-        for q in range(4):
-            nc.scalar.dma_start(out=b_rows[32 * q : 32 * q + M_TILES, :], in_=b_view[q])
+        load_w(0, 1)
+        b_bank = psum.tile([P, N], F32, name="b_bank", tag="acc")
+        nc.tensor.transpose(b_bank[:, 0:P], b_rows[:], identity[:])
+        nc.scalar.copy(b_cols[:], b_bank[:, 0:M_TILES])
 
-        chunks = [(0, 256), (256, 256), (512, 512)]
-        w_raw = {}
-        for k, (c0, width) in enumerate(chunks):
-            for a in range(PASSES):
-                raw = keep.tile([P, 4, width], F32, name=f"raw{k}{a}")
-                nc.vector.memset(raw[:, 0, 0:1], 0.0)
-                nc.sync.dma_start(
-                    out=raw[:],
-                    in_=w[512 * a : 512 * a + 512, c0 : c0 + width].rearrange("(p i) c -> p i c", i=4),
-                )
-                w_raw[k, a] = raw
-        nc.vector.transpose(b_cols[:], b_rows[:])
-
-        g_words, g_scales, parted = {}, {}, {}
         w_codes = keep.tile([P, PASSES, M], U32, name="w_codes", align_bytes=64)
         w_scales = keep.tile([P, PASSES, M], U8, name="w_scales", align_bytes=64)
-        outs = {}
-        for m in range(M_TILES):
-            outs[m] = keep.tile([P, S], F32, name=f"outs{m}")
+        outs = [keep.tile([P, S], F32, name=f"outs{m}") for m in range(M_TILES)]
+        parted = [keep.tile([P, PASSES, 2 * N], U8, name=f"parted{s}", align_bytes=64) for s in range(SLICES)]
 
-        def list_of(s):
-            return offsets[:, s * (N // 16) : (s + 1) * (N // 16)]
-
-        scale_tags = {0: "sc0", 1: "sc1", 2: "turn01a", 3: "turn21a"}
-        word_tags = {0: "gw0", 1: "turn01b", 2: "turn11", 3: "turn21b"}
-
-        def gather_scales(s):
-            g = keep.tile([P, PASSES, N], U8, name=f"g_scales{s}", tag=scale_tags[s], align_bytes=64)
-            for h in range(PASSES):
-                nc.vector.tensor_copy(g[:, h, :], planes[:, h, :].indirect(list_of(s)))
-            g_scales[s] = g
+        def gather_scales(i):
+            cols = N_SCALES // 16
+            nc.vector.tensor_copy(first[i][:], plane[:].indirect(offsets[:, i * cols : (i + 1) * cols]))
+            nc.sync.dma_start(
+                out=second[i][0 : P - SHIFT, :].bitcast(I32), in_=first[i][SHIFT:P, :].bitcast(I32)
+            )
 
         def gather_words(s):
-            g = keep.tile([P, N], I32, name=f"g_words{s}", tag=word_tags[s], align_bytes=64)
-            nc.vector.tensor_copy(g[:].bitcast(U32), words[:].bitcast(U32).indirect(list_of(s)))
-            g_words[s] = g
-
-        def part(s):
-            t = keep.tile([P, PASSES, 2 * N], U8, name=f"parted{s}", align_bytes=64)
+            cols = N // 16
+            g = keep.tile([P, N], I32, name=f"g_words{s}", tag=("g_words", "turn010", "g_words", "turn010")[s], align_bytes=64)
             nc.vector.tensor_copy(
-                t[:].rearrange("p h c -> p (h c)").bitcast(U16).rearrange("p (h n) -> p h n", h=PASSES),
-                g_words[s][:].bitcast(U16).rearrange("p (n h) -> p h n", h=PASSES),
+                g[:].bitcast(U32), words[:].bitcast(U32).indirect(offsets[:, s * cols : (s + 1) * cols])
             )
-            parted[s] = t
+            nc.vector.tensor_copy(
+                parted[s][:].rearrange("p h c -> p (h c)").bitcast(U16).rearrange("p (h n) -> p h n", h=PASSES),
+                g[:].bitcast(U16).rearrange("p (n h) -> p h n", h=PASSES),
+            )
 
         grouped = {}
 
-        def group(engine, k, a, c0, c1, tag):
-            t = keep.tile([P, c1 - c0, 4], BF16, name=f"grouped{k}{a}{c0}", tag=tag, align_bytes=64)
-            src = w_raw[k, a][:, :, c0:c1].rearrange("p i c -> p c i")
+        def group(engine, half, a, c0, c1):
+            t = keep.tile([P, c1 - c0, 4], BF16, name=f"grouped{half}{a}{c0}", tag=f"turn{half}{a}{c0}", align_bytes=64)
+            src = raws[half, a][:, :, c0:c1].rearrange("p i c -> p c i")
             if engine == "scalar":
                 nc.scalar.copy(t[:], src)
-            elif engine == "gpsimd":
-                nc.gpsimd.tensor_copy(t[:], src)
             else:
                 nc.vector.tensor_copy(t[:], src)
-            grouped[k, a, c0] = t
+            grouped[half, a, c0] = t
 
-        def quantize(k, a, c0, c1):
-            cols = slice(chunks[k][0] + c0, chunks[k][0] + c1)
+        def quantize(half, a, c0, c1):
+            cols = slice(HALF * half + c0, HALF * half + c1)
             nc.vector.quantize_mx(
                 out=w_codes[:, a, cols].bitcast(E4M3),
                 scales=w_scales[:, a, cols],
-                in_=grouped[k, a, c0][:].rearrange("p c i -> p (c i)"),
+                in_=grouped[half, a, c0][:].rearrange("p c i -> p (c i)"),
             )
 
         def product(m, s, step=N):
-            acc = psum.tile([P, N], F32, name="acc")
+            acc = psum.tile([P, N], F32, name="acc", tag="acc")
+            i, c0 = divmod(N * s, N_SCALES)
             for a in range(PASSES):
                 nc.tensor.matmul_mx(
                     out=acc[:],
                     lhsT=w_codes[:, a, P * m : P * m + P].bitcast(E4M3),
                     lhsT_scale=w_scales[:, a, P * m : P * m + P],
                     rhs=parted[s][:, a, :].bitcast(E2M1),
-                    rhs_scale=g_scales[s][:, a, :],
+                    rhs_scale=(first, second)[a][i][:, c0 : c0 + N],
                     start=(a == 0),
                     stop=(a == PASSES - 1),
                 )
@@ -145,60 +147,37 @@ def tile_list_tab4_gelu_kernel(tc, tab, w, b, offs, out):
             nc.sync.dma_start(out=out[P * m : P * m + P, c0:c1], in_=outs[m][:, c0:c1])
 
         gather_scales(0)
-        group("scalar", 0, 0, 0, 256, "turn00")
-        group("scalar", 0, 1, 0, 128, "turn01a")
-        group("gpsimd", 0, 1, 128, 256, "turn01b")
-        group("gpsimd", 1, 0, 0, 256, "turn10")
-        group("gpsimd", 1, 1, 0, 256, "turn11")
-        group("gpsimd", 2, 0, 0, 256, "turn20a")
-        group("gpsimd", 2, 0, 256, 512, "turn20b")
-        group("gpsimd", 2, 1, 256, 512, "turn21b")
-        gather_words(0)
-        part(0)
-        quantize(0, 0, 0, 256)
-        quantize(0, 1, 0, 128)
-        quantize(0, 1, 128, 256)
-        for m in range(2):
-            product(m, 0)
+        for a in range(PASSES):
+            group("scalar", 0, a, 0, 256)
+            group("scalar", 0, a, 256, 512)
         gather_scales(1)
-        gather_words(1)
-        part(1)
-        for m in range(2):
-            product(m, 1)
-            store(m, 0, 1024)
-        quantize(1, 0, 0, 256)
-        quantize(1, 1, 0, 256)
-        for m in range(2, 4):
-            product(m, 0)
-            product(m, 1)
-            store(m, 0, 1024)
-        gather_scales(2)
-        gather_words(2)
-        part(2)
+        late = keep.tile([P, PASSES, 4, HALF], F32, name="late", tag="plane", align_bytes=64)
+        for a in range(PASSES):
+            raws[1, a] = late[:, a, :, :]
+            load_w(1, a)
+        gather_words(0)
+        for c0 in (0, 256):
+            for a in range(PASSES):
+                quantize(0, a, c0, c0 + 256)
         for m in range(4):
-            product(m, 2)
-        group("vector", 2, 1, 0, 256, "turn21a")
-        quantize(2, 0, 0, 256)
-        quantize(2, 1, 0, 256)
-        quantize(2, 0, 256, 512)
-        quantize(2, 1, 256, 512)
-        for m in range(4, 8):
             product(m, 0)
-            product(m, 1)
-            store(m, 0, 1024)
-        gather_scales(3)
-        gather_words(3)
-        part(3)
-        for m in range(4):
-            product(m, 3)
-            store(m, 1024, 2048)
+        for s in (1, 2, 3):
+            gather_words(s)
+            for m in range(4):
+                product(m, s)
+                if s % 2:
+                    store(m, N * (s - 1), N * (s + 1))
+        for c0 in (0, 256):
+            for a in range(PASSES):
+                group("vector", 1, a, c0, c0 + 256)
+            for a in range(PASSES):
+                quantize(1, a, c0, c0 + 256)
         for m in range(4, 8):
-            product(m, 2)
-            if m < 7:
-                product(m, 3)
-                store(m, 1024, 2048)
-            else:
-                store(m, 1024, 1536)
-                product(m, 3, step=256)
-                store(m, 1536, 1792)
-                store(m, 1792, 2048)
+            for s in range(SLICES):
+                last = m == 7 and s == 3
+                product(m, s, step=256 if last else N)
+                if m == 7 and s >= 2:
+                    for c in range(N * s, N * s + N, 256 if last else N):
+                        store(m, c, c + (256 if last else N))
+                elif s % 2:
+                    store(m, N * (s - 1), N * (s + 1))

@@ -42,46 +42,41 @@ def tile_list_tab4_gelu_kernel(tc, tab, w, b, offs, out):
         first = [keep.tile([P, N_SCALES], U8, name=f"first{i}", align_bytes=64) for i in range(2)]
         second = [keep.tile([P, N_SCALES], U8, name=f"second{i}", align_bytes=64) for i in range(2)]
         raws = {}
-        for a in range(PASSES):
-            raws[0, a] = keep.tile([P, 4, HALF], F32, name=f"raw{a}")[:]
 
-        def load_w(half, a):
+        chunks = [(0, 256), (256, 256), (512, 512)]
+
+        def load_w(k, a):
+            c0, width = chunks[k]
             nc.sync.dma_start(
-                out=raws[half, a],
-                in_=w[512 * a : 512 * a + 512, HALF * half : HALF * half + HALF].rearrange("(p i) c -> p i c", i=4),
+                out=raws[k][:, a, :, :],
+                in_=w[512 * a : 512 * a + 512, c0 : c0 + width].rearrange("(p i) c -> p i c", i=4),
             )
 
+        raws[0] = keep.tile([P, PASSES, 4, 256], F32, name="raw0")
         nc.sync.dma_start(offsets[:], offs)
         load_w(0, 0)
+        load_w(0, 1)
 
         nc.vector.memset(plane[:].bitcast(I32), 0)
         nc.vector.memset(words[:, 0:1], 0)
-        nc.vector.memset(raws[0, 1][:, 0, 0:1], 0.0)
-        nc.vector.memset(warm[:], 0.0)
         nc.gpsimd.memset(b_rows[:], 0.0)
+        nc.scalar.dma_start(out=b_rows[0:M_TILES, :], in_=b.rearrange("(j p) -> j p", p=P))
         make_identity(nc, identity[:])
         for i in range(2):
             nc.gpsimd.memset(second[i][:].bitcast(I32), 0)
-        nc.scalar.dma_start(out=b_rows[0:M_TILES, :], in_=b.rearrange("(j p) -> j p", p=P))
-        nc.scalar.activation(warm[:], warm[:], GELU)
 
         scale_rows = tab[0, 512 * T : 544 * T].rearrange("(q t) -> q t", t=T)
-        for h in range(PASSES):
-            queue = nc.sync if h == 0 else nc.gpsimd
-            for q in range(4):
-                p0 = 32 * q + SHIFT * h
-                queue.dma_start(
-                    out=plane[p0 : p0 + 4, :].bitcast(I32),
-                    in_=scale_rows[16 * h + 4 * q : 16 * h + 4 * q + 4, :].bitcast(I32),
-                )
+        for q in range(4):
+            nc.sync.dma_start(
+                out=plane[32 * q : 32 * q + SHIFT + 4, :].bitcast(I32),
+                in_=scale_rows[4 * q : 4 * q + SHIFT + 4, :].bitcast(I32),
+            )
         nc.sync.dma_start(
             out=words[:],
             in_=tab[0, 0 : 512 * T].rearrange("(p c) -> p c", p=P).bitcast(I32),
         )
-        load_w(0, 1)
-        b_bank = psum.tile([P, N], F32, name="b_bank", tag="acc")
-        nc.tensor.transpose(b_bank[:, 0:P], b_rows[:], identity[:])
-        nc.scalar.copy(b_cols[:], b_bank[:, 0:M_TILES])
+        nc.vector.memset(warm[:], 0.0)
+        nc.scalar.activation(warm[:], warm[:], GELU)
 
         w_codes = keep.tile([P, PASSES, M], U32, name="w_codes", align_bytes=64)
         w_scales = keep.tile([P, PASSES, M], U8, name="w_scales", align_bytes=64)
@@ -97,7 +92,7 @@ def tile_list_tab4_gelu_kernel(tc, tab, w, b, offs, out):
 
         def gather_words(s):
             cols = N // 16
-            g = keep.tile([P, N], I32, name=f"g_words{s}", tag=("g_words", "turn010", "g_words", "turn010")[s], align_bytes=64)
+            g = keep.tile([P, N], I32, name=f"g_words{s}", tag=("g_words", "turn010", "turn110", "turn110")[s], align_bytes=64)
             nc.vector.tensor_copy(
                 g[:].bitcast(U32), words[:].bitcast(U32).indirect(offsets[:, s * cols : (s + 1) * cols])
             )
@@ -108,21 +103,21 @@ def tile_list_tab4_gelu_kernel(tc, tab, w, b, offs, out):
 
         grouped = {}
 
-        def group(engine, half, a, c0, c1):
-            t = keep.tile([P, c1 - c0, 4], BF16, name=f"grouped{half}{a}{c0}", tag=f"turn{half}{a}{c0}", align_bytes=64)
-            src = raws[half, a][:, :, c0:c1].rearrange("p i c -> p c i")
+        def group(engine, k, a, c0):
+            t = keep.tile([P, 256, 4], BF16, name=f"grouped{k}{a}{c0}", tag=f"turn{k}{a}{c0}", align_bytes=64)
+            src = raws[k][:, a, :, c0 : c0 + 256].rearrange("p i c -> p c i")
             if engine == "scalar":
                 nc.scalar.copy(t[:], src)
             else:
                 nc.vector.tensor_copy(t[:], src)
-            grouped[half, a, c0] = t
+            grouped[k, a, c0] = t
 
-        def quantize(half, a, c0, c1):
-            cols = slice(HALF * half + c0, HALF * half + c1)
+        def quantize(k, a, c0):
+            cols = slice(chunks[k][0] + c0, chunks[k][0] + c0 + 256)
             nc.vector.quantize_mx(
                 out=w_codes[:, a, cols].bitcast(E4M3),
                 scales=w_scales[:, a, cols],
-                in_=grouped[half, a, c0][:].rearrange("p c i -> p (c i)"),
+                in_=grouped[k, a, c0][:].rearrange("p c i -> p (c i)"),
             )
 
         def product(m, s, step=N):
@@ -146,32 +141,48 @@ def tile_list_tab4_gelu_kernel(tc, tab, w, b, offs, out):
         def store(m, c0, c1):
             nc.sync.dma_start(out=out[P * m : P * m + P, c0:c1], in_=outs[m][:, c0:c1])
 
+        group("scalar", 0, 0, 0)
+        group("scalar", 0, 1, 0)
+        b_bank = psum.tile([P, N], F32, name="b_bank", tag="acc")
+        nc.tensor.transpose(b_bank[:, 0:P], b_rows[:], identity[:])
+        nc.scalar.copy(b_cols[:], b_bank[:, 0:M_TILES])
         gather_scales(0)
-        for a in range(PASSES):
-            group("scalar", 0, a, 0, 256)
-            group("scalar", 0, a, 256, 512)
+        quantize(0, 0, 0)
+        quantize(0, 1, 0)
+        raws[1] = keep.tile([P, PASSES, 4, 256], F32, name="raw1", tag="turn000", align_bytes=64)
+        load_w(1, 0)
+        load_w(1, 1)
         gather_scales(1)
-        late = keep.tile([P, PASSES, 4, HALF], F32, name="late", tag="plane", align_bytes=64)
-        for a in range(PASSES):
-            raws[1, a] = late[:, a, :, :]
-            load_w(1, a)
+        raws[2] = keep.tile([P, PASSES, 4, 512], F32, name="raw2", tag="plane", align_bytes=64)
+        load_w(2, 0)
+        load_w(2, 1)
         gather_words(0)
-        for c0 in (0, 256):
-            for a in range(PASSES):
-                quantize(0, a, c0, c0 + 256)
-        for m in range(4):
+        group("scalar", 1, 0, 0)
+        for m in range(2):
             product(m, 0)
-        for s in (1, 2, 3):
+            store(m, 0, N)
+        gather_words(1)
+        for m in range(2):
+            product(m, 1)
+            store(m, N, 2 * N)
+        group("vector", 1, 1, 0)
+        quantize(1, 0, 0)
+        quantize(1, 1, 0)
+        for m in range(2, 4):
+            product(m, 0)
+            product(m, 1)
+            store(m, 0, 2 * N)
+        for s in (2, 3):
             gather_words(s)
             for m in range(4):
                 product(m, s)
-                if s % 2:
-                    store(m, N * (s - 1), N * (s + 1))
+                if s == 3:
+                    store(m, 2 * N, 4 * N)
         for c0 in (0, 256):
             for a in range(PASSES):
-                group("vector", 1, a, c0, c0 + 256)
+                group("vector", 2, a, c0)
             for a in range(PASSES):
-                quantize(1, a, c0, c0 + 256)
+                quantize(2, a, c0)
         for m in range(4, 8):
             for s in range(SLICES):
                 last = m == 7 and s == 3

@@ -17,13 +17,19 @@ E2M1 = mybir.dt.float4_e2m1fn_x4
 GELU = mybir.ActivationFunctionType.Gelu_apprx_tanh
 
 P = 128
-PASSES = 2
-N = 512
-SLICES = S // N
-HALF = 512
+QUAD = 32
+PACK = 4
+PASSES = K // (P * PACK)
+SCALE_ROWS = K // 32
 M_TILES = M // P
-SHIFT = 16
-N_SCALES = 1024
+
+N = 512
+RUN = 1024
+PIECE = 256
+CHUNKS = [(0, 256), (256, 256), (512, 512)]
+
+SHIFTS = (QUAD - 4 - SCALE_ROWS // PASSES, QUAD - 4)
+MOVED = (112, 100)
 
 
 def tile_list_tab4_gelu_kernel(tc, tab, w, b, offs, out):
@@ -34,161 +40,151 @@ def tile_list_tab4_gelu_kernel(tc, tab, w, b, offs, out):
 
         offsets = keep.tile([P, S // 16], U16, name="offsets")
         words = keep.tile([P, T], I32, name="words")
-        plane = keep.tile([P, T], U8, name="plane", tag="plane", align_bytes=64)
+        table_scales = keep.tile([P, T], U8, name="table_scales", align_bytes=64)
         b_rows = keep.tile([P, P], F32, name="b_rows")
         b_cols = keep.tile([P, M_TILES], F32, name="b_cols")
         identity = keep.tile([P, P], F32, name="identity")
         warm = keep.tile([P, 1], F32, name="warm")
-        first = [keep.tile([P, N_SCALES], U8, name=f"first{i}", align_bytes=64) for i in range(2)]
-        second = [keep.tile([P, N_SCALES], U8, name=f"second{i}", align_bytes=64) for i in range(2)]
-        raws = {}
+        scales = [
+            [keep.tile([P, RUN], U8, name=f"scales{r}{h}", align_bytes=64) for h in range(PASSES)]
+            for r in range(S // RUN)
+        ]
+        parted = [keep.tile([P, PASSES, 2 * N], U8, name=f"parted{s}", align_bytes=64) for s in range(S // N)]
+        results = [keep.tile([P, S], F32, name=f"results{m}") for m in range(M_TILES)]
+        raws, grouped, codes, code_scales = {}, {}, {}, {}
 
-        chunks = [(0, 256), (256, 256), (512, 512)]
+        def load_w(k, tag):
+            c0, width = CHUNKS[k]
+            raws[k] = keep.tile([P, PASSES, PACK, width], F32, name=f"raw{k}", tag=tag, align_bytes=64)
+            for a in range(PASSES):
+                rows = w[P * PACK * a : P * PACK * (a + 1), c0 : c0 + width]
+                nc.sync.dma_start(out=raws[k][:, a, :, :], in_=rows.rearrange("(p i) c -> p i c", i=PACK))
 
-        def load_w(k, a):
-            c0, width = chunks[k]
-            nc.sync.dma_start(
-                out=raws[k][:, a, :, :],
-                in_=w[512 * a : 512 * a + 512, c0 : c0 + width].rearrange("(p i) c -> p i c", i=4),
-            )
+        def group(copy, i, a):
+            k = max(j for j in range(len(CHUNKS)) if CHUNKS[j][0] <= PIECE * i)
+            c0 = PIECE * i - CHUNKS[k][0]
+            if i not in grouped:
+                grouped[i] = keep.tile([P, PASSES, PIECE, PACK], BF16, name=f"grouped{i}", tag=f"turn{i}", align_bytes=64)
+            copy(grouped[i][:, a, :, :], raws[k][:, a, :, c0 : c0 + PIECE].rearrange("p i c -> p c i"))
 
-        raws[0] = keep.tile([P, PASSES, 4, 256], F32, name="raw0")
-        nc.sync.dma_start(offsets[:], offs)
-        load_w(0, 0)
-        load_w(0, 1)
-
-        nc.vector.memset(plane[:].bitcast(I32), 0)
-        nc.vector.memset(words[:, 0:1], 0)
-        nc.gpsimd.memset(b_rows[:], 0.0)
-        nc.scalar.dma_start(out=b_rows[0:M_TILES, :], in_=b.rearrange("(j p) -> j p", p=P))
-        make_identity(nc, identity[:])
-        for i in range(2):
-            nc.gpsimd.memset(second[i][:].bitcast(I32), 0)
-
-        scale_rows = tab[0, 512 * T : 544 * T].rearrange("(q t) -> q t", t=T)
-        for q in range(4):
-            nc.sync.dma_start(
-                out=plane[32 * q : 32 * q + SHIFT + 4, :].bitcast(I32),
-                in_=scale_rows[4 * q : 4 * q + SHIFT + 4, :].bitcast(I32),
-            )
-        nc.sync.dma_start(
-            out=words[:],
-            in_=tab[0, 0 : 512 * T].rearrange("(p c) -> p c", p=P).bitcast(I32),
-        )
-        nc.vector.memset(warm[:], 0.0)
-        nc.scalar.activation(warm[:], warm[:], GELU)
-
-        w_codes = keep.tile([P, PASSES, M], U32, name="w_codes", align_bytes=64)
-        w_scales = keep.tile([P, PASSES, M], U8, name="w_scales", align_bytes=64)
-        outs = [keep.tile([P, S], F32, name=f"outs{m}") for m in range(M_TILES)]
-        parted = [keep.tile([P, PASSES, 2 * N], U8, name=f"parted{s}", align_bytes=64) for s in range(SLICES)]
-
-        def gather_scales(i):
-            cols = N_SCALES // 16
-            nc.vector.tensor_copy(first[i][:], plane[:].indirect(offsets[:, i * cols : (i + 1) * cols]))
-            nc.sync.dma_start(
-                out=second[i][0 : P - SHIFT, :].bitcast(I32), in_=first[i][SHIFT:P, :].bitcast(I32)
-            )
-
-        def gather_words(s):
-            cols = N // 16
-            g = keep.tile([P, N], I32, name=f"g_words{s}", tag=("g_words", "turn010", "turn110", "turn110")[s], align_bytes=64)
-            nc.vector.tensor_copy(
-                g[:].bitcast(U32), words[:].bitcast(U32).indirect(offsets[:, s * cols : (s + 1) * cols])
-            )
-            nc.vector.tensor_copy(
-                parted[s][:].rearrange("p h c -> p (h c)").bitcast(U16).rearrange("p (h n) -> p h n", h=PASSES),
-                g[:].bitcast(U16).rearrange("p (n h) -> p h n", h=PASSES),
-            )
-
-        grouped = {}
-
-        def group(engine, k, a, c0):
-            t = keep.tile([P, 256, 4], BF16, name=f"grouped{k}{a}{c0}", tag=f"turn{k}{a}{c0}", align_bytes=64)
-            src = raws[k][:, a, :, c0 : c0 + 256].rearrange("p i c -> p c i")
-            if engine == "scalar":
-                nc.scalar.copy(t[:], src)
-            else:
-                nc.vector.tensor_copy(t[:], src)
-            grouped[k, a, c0] = t
-
-        def quantize(k, a, c0):
-            cols = slice(chunks[k][0] + c0, chunks[k][0] + c0 + 256)
+        def quantize(i):
+            codes[i] = keep.tile([P, PASSES, PIECE], U32, name=f"codes{i}", align_bytes=64)
+            code_scales[i] = keep.tile([P, PASSES, PIECE], U8, name=f"code_scales{i}", align_bytes=64)
             nc.vector.quantize_mx(
-                out=w_codes[:, a, cols].bitcast(E4M3),
-                scales=w_scales[:, a, cols],
-                in_=grouped[k, a, c0][:].rearrange("p c i -> p (c i)"),
+                out=codes[i][:].rearrange("p a c -> p (a c)").bitcast(E4M3),
+                scales=code_scales[i][:].rearrange("p a c -> p (a c)"),
+                in_=grouped[i][:].rearrange("p a c i -> p (a c i)"),
+            )
+
+        def gather_scales(r):
+            picked = keep.tile([P, RUN], U8, name=f"picked{r}", align_bytes=64)
+            cols = slice(r * RUN // 16, (r + 1) * RUN // 16)
+            nc.vector.tensor_copy(picked[:], table_scales[:].indirect(offsets[:, cols]))
+            for h in range(PASSES):
+                nc.sync.dma_start(
+                    out=scales[r][h][0 : MOVED[h], :].bitcast(I32),
+                    in_=picked[SHIFTS[h] : SHIFTS[h] + MOVED[h], :].bitcast(I32),
+                )
+
+        def gather_words(s, tag):
+            picked = keep.tile([P, N], I32, name=f"picked_words{s}", tag=tag, align_bytes=64)
+            cols = slice(s * N // 16, (s + 1) * N // 16)
+            nc.vector.tensor_copy(picked[:].bitcast(U32), words[:].bitcast(U32).indirect(offsets[:, cols]))
+            halves = parted[s][:].rearrange("p h c -> p (h c)").bitcast(U16)
+            nc.vector.tensor_copy(
+                halves.rearrange("p (h n) -> p h n", h=PASSES),
+                picked[:].bitcast(U16).rearrange("p (n h) -> p h n", h=PASSES),
             )
 
         def product(m, s, step=N):
             acc = psum.tile([P, N], F32, name="acc", tag="acc")
-            i, c0 = divmod(N * s, N_SCALES)
+            piece, m0 = divmod(P * m, PIECE)
+            r, j0 = divmod(N * s, RUN)
             for a in range(PASSES):
                 nc.tensor.matmul_mx(
                     out=acc[:],
-                    lhsT=w_codes[:, a, P * m : P * m + P].bitcast(E4M3),
-                    lhsT_scale=w_scales[:, a, P * m : P * m + P],
+                    lhsT=codes[piece][:, a, m0 : m0 + P].bitcast(E4M3),
+                    lhsT_scale=code_scales[piece][:, a, m0 : m0 + P],
                     rhs=parted[s][:, a, :].bitcast(E2M1),
-                    rhs_scale=(first, second)[a][i][:, c0 : c0 + N],
+                    rhs_scale=scales[r][a][:, j0 : j0 + N],
                     start=(a == 0),
                     stop=(a == PASSES - 1),
                 )
             for c in range(0, N, step):
                 nc.scalar.activation(
-                    outs[m][:, N * s + c : N * s + c + step], acc[:, c : c + step], GELU, bias=b_cols[:, m : m + 1]
+                    results[m][:, N * s + c : N * s + c + step], acc[:, c : c + step], GELU, bias=b_cols[:, m : m + 1]
                 )
 
         def store(m, c0, c1):
-            nc.sync.dma_start(out=out[P * m : P * m + P, c0:c1], in_=outs[m][:, c0:c1])
+            nc.sync.dma_start(out=out[P * m : P * m + P, c0:c1], in_=results[m][:, c0:c1])
 
-        group("scalar", 0, 0, 0)
-        group("scalar", 0, 1, 0)
+        nc.sync.dma_start(offsets[:], offs)
+        for q in range(P // QUAD):
+            row0 = 4 * q - SHIFTS[0]
+            start = 512 * T + T * row0
+            nc.sync.dma_start(
+                out=table_scales[QUAD * q : QUAD * (q + 1), :].bitcast(I32),
+                in_=tab[0, start : start + QUAD * T].rearrange("(r t) -> r t", t=T).bitcast(I32),
+            )
+        load_w(0, "raw")
+        nc.sync.dma_start(out=words[:], in_=tab[0, 0 : 512 * T].rearrange("(p c) -> p c", p=P).bitcast(I32))
+
+        nc.vector.memset(warm[:], 0.0)
+        nc.scalar.activation(warm[:], warm[:], GELU)
+        nc.gpsimd.memset(b_rows[:], 0.0)
+        nc.scalar.dma_start(out=b_rows[0:M_TILES, :], in_=b.rearrange("(m p) -> m p", p=P))
+        make_identity(nc, identity[:])
+        for r in range(S // RUN):
+            for h in range(PASSES):
+                nc.gpsimd.memset(scales[r][h][:].bitcast(I32), 0)
+
+        for a in range(PASSES):
+            group(nc.scalar.copy, 0, a)
         b_bank = psum.tile([P, N], F32, name="b_bank", tag="acc")
         nc.tensor.transpose(b_bank[:, 0:P], b_rows[:], identity[:])
         nc.scalar.copy(b_cols[:], b_bank[:, 0:M_TILES])
+
         gather_scales(0)
-        quantize(0, 0, 0)
-        quantize(0, 1, 0)
-        raws[1] = keep.tile([P, PASSES, 4, 256], F32, name="raw1", tag="turn000", align_bytes=64)
-        load_w(1, 0)
-        load_w(1, 1)
+        load_w(1, "raw")
+        quantize(0)
         gather_scales(1)
-        raws[2] = keep.tile([P, PASSES, 4, 512], F32, name="raw2", tag="plane", align_bytes=64)
-        load_w(2, 0)
-        load_w(2, 1)
-        gather_words(0)
-        group("scalar", 1, 0, 0)
-        for m in range(2):
+        load_w(2, "turn0")
+        gather_words(0, "words01")
+        group(nc.scalar.copy, 1, 0)
+        for m in (0, 1):
             product(m, 0)
             store(m, 0, N)
-        gather_words(1)
-        for m in range(2):
+        gather_words(1, "words01")
+        for m in (0, 1):
             product(m, 1)
             store(m, N, 2 * N)
-        group("vector", 1, 1, 0)
-        quantize(1, 0, 0)
-        quantize(1, 1, 0)
-        for m in range(2, 4):
+        group(nc.vector.tensor_copy, 1, 1)
+        quantize(1)
+        for m in (2, 3):
             product(m, 0)
             product(m, 1)
             store(m, 0, 2 * N)
-        for s in (2, 3):
-            gather_words(s)
-            for m in range(4):
-                product(m, s)
-                if s == 3:
-                    store(m, 2 * N, 4 * N)
-        for c0 in (0, 256):
+        gather_words(2, "turn1")
+        for m in range(4):
+            product(m, 2)
+        gather_words(3, "turn1")
+        for m in range(4):
+            product(m, 3)
+            store(m, 2 * N, 4 * N)
+        for i in (2, 3):
             for a in range(PASSES):
-                group("vector", 2, a, c0)
-            for a in range(PASSES):
-                quantize(2, a, c0)
-        for m in range(4, 8):
-            for s in range(SLICES):
-                last = m == 7 and s == 3
-                product(m, s, step=256 if last else N)
-                if m == 7 and s >= 2:
-                    for c in range(N * s, N * s + N, 256 if last else N):
-                        store(m, c, c + (256 if last else N))
-                elif s % 2:
-                    store(m, N * (s - 1), N * (s + 1))
+                group(nc.vector.tensor_copy, i, a)
+            quantize(i)
+        for m in range(4, M_TILES):
+            product(m, 0)
+            product(m, 1)
+            store(m, 0, 2 * N)
+            product(m, 2)
+            if m < M_TILES - 1:
+                product(m, 3)
+                store(m, 2 * N, 4 * N)
+        m, half = M_TILES - 1, N // 2
+        store(m, 2 * N, 3 * N)
+        product(m, 3, step=half)
+        store(m, 3 * N, 3 * N + half)
+        store(m, 3 * N + half, 4 * N)

from contextlib import ExitStack

import concourse.mybir as mybir
from concourse.masks import make_identity

K, M, T, S = 1024, 1024, 4096, 2048
FLOPS = 2 * K * M * S

F32 = mybir.dt.float32
BF16 = mybir.dt.bfloat16
I32 = mybir.dt.int32
U32 = mybir.dt.uint32
U16 = mybir.dt.uint16
U8 = mybir.dt.uint8
E4M3 = mybir.dt.float8_e4m3fn_x4
E2M1 = mybir.dt.float4_e2m1fn_x4
GELU = mybir.ActivationFunctionType.Gelu_apprx_tanh

P = 128
QUAD = 32
PACK = 4
PASSES = K // (P * PACK)
SCALE_ROWS = K // 32
M_TILES = M // P

N = 512
RUN = 1024
PIECE = 256
CHUNKS = [(0, 256), (256, 256), (512, 512)]

SHIFTS = (QUAD - 4 - SCALE_ROWS // PASSES, QUAD - 4)
MOVED = (112, 100)


def tile_list_tab4_gelu_kernel(tc, tab, w, b, offs, out):
    nc = tc.nc
    with ExitStack() as ctx:
        keep = ctx.enter_context(tc.tile_pool(name="keep", bufs=1))
        psum = ctx.enter_context(tc.psum_pool(name="psum", bufs=8))

        offsets = keep.tile([P, S // 16], U16, name="offsets")
        words = keep.tile([P, T], I32, name="words")
        table_scales = keep.tile([P, T], U8, name="table_scales", align_bytes=64)
        b_rows = keep.tile([P, P], F32, name="b_rows")
        b_cols = keep.tile([P, M_TILES], F32, name="b_cols")
        identity = keep.tile([P, P], F32, name="identity")
        warm = keep.tile([P, 1], F32, name="warm")
        scales = [
            [keep.tile([P, RUN], U8, name=f"scales{r}{h}", align_bytes=64) for h in range(PASSES)]
            for r in range(S // RUN)
        ]
        parted = [keep.tile([P, PASSES, 2 * N], U8, name=f"parted{s}", align_bytes=64) for s in range(S // N)]
        results = [keep.tile([P, S], F32, name=f"results{m}") for m in range(M_TILES)]
        raws, grouped, codes, code_scales = {}, {}, {}, {}

        def load_w(k, tag):
            c0, width = CHUNKS[k]
            raws[k] = keep.tile([P, PASSES, PACK, width], F32, name=f"raw{k}", tag=tag, align_bytes=64)
            for a in range(PASSES):
                rows = w[P * PACK * a : P * PACK * (a + 1), c0 : c0 + width]
                nc.sync.dma_start(out=raws[k][:, a, :, :], in_=rows.rearrange("(p i) c -> p i c", i=PACK))

        def group(copy, i, a):
            k = max(j for j in range(len(CHUNKS)) if CHUNKS[j][0] <= PIECE * i)
            c0 = PIECE * i - CHUNKS[k][0]
            if i not in grouped:
                grouped[i] = keep.tile([P, PASSES, PIECE, PACK], BF16, name=f"grouped{i}", tag=f"turn{i}", align_bytes=64)
            copy(grouped[i][:, a, :, :], raws[k][:, a, :, c0 : c0 + PIECE].rearrange("p i c -> p c i"))

        def quantize(i):
            codes[i] = keep.tile([P, PASSES, PIECE], U32, name=f"codes{i}", align_bytes=64)
            code_scales[i] = keep.tile([P, PASSES, PIECE], U8, name=f"code_scales{i}", align_bytes=64)
            nc.vector.quantize_mx(
                out=codes[i][:].rearrange("p a c -> p (a c)").bitcast(E4M3),
                scales=code_scales[i][:].rearrange("p a c -> p (a c)"),
                in_=grouped[i][:].rearrange("p a c i -> p (a c i)"),
            )

        def gather_scales(r):
            picked = keep.tile([P, RUN], U8, name=f"picked{r}", align_bytes=64)
            cols = slice(r * RUN // 16, (r + 1) * RUN // 16)
            nc.vector.tensor_copy(picked[:], table_scales[:].indirect(offsets[:, cols]))
            for h in range(PASSES):
                nc.sync.dma_start(
                    out=scales[r][h][0 : MOVED[h], :].bitcast(I32),
                    in_=picked[SHIFTS[h] : SHIFTS[h] + MOVED[h], :].bitcast(I32),
                )

        def gather_words(s, tag):
            picked = keep.tile([P, N], I32, name=f"picked_words{s}", tag=tag, align_bytes=64)
            cols = slice(s * N // 16, (s + 1) * N // 16)
            nc.vector.tensor_copy(picked[:].bitcast(U32), words[:].bitcast(U32).indirect(offsets[:, cols]))
            halves = parted[s][:].rearrange("p h c -> p (h c)").bitcast(U16)
            nc.vector.tensor_copy(
                halves.rearrange("p (h n) -> p h n", h=PASSES),
                picked[:].bitcast(U16).rearrange("p (n h) -> p h n", h=PASSES),
            )

        def product(m, s, step=N):
            acc = psum.tile([P, N], F32, name="acc", tag="acc")
            piece, m0 = divmod(P * m, PIECE)
            r, j0 = divmod(N * s, RUN)
            for a in range(PASSES):
                nc.tensor.matmul_mx(
                    out=acc[:],
                    lhsT=codes[piece][:, a, m0 : m0 + P].bitcast(E4M3),
                    lhsT_scale=code_scales[piece][:, a, m0 : m0 + P],
                    rhs=parted[s][:, a, :].bitcast(E2M1),
                    rhs_scale=scales[r][a][:, j0 : j0 + N],
                    start=(a == 0),
                    stop=(a == PASSES - 1),
                )
            for c in range(0, N, step):
                nc.scalar.activation(
                    results[m][:, N * s + c : N * s + c + step], acc[:, c : c + step], GELU, bias=b_cols[:, m : m + 1]
                )

        def store(m, c0, c1):
            nc.sync.dma_start(out=out[P * m : P * m + P, c0:c1], in_=results[m][:, c0:c1])

        nc.sync.dma_start(offsets[:], offs)
        for q in range(P // QUAD):
            row0 = 4 * q - SHIFTS[0]
            start = 512 * T + T * row0
            nc.sync.dma_start(
                out=table_scales[QUAD * q : QUAD * (q + 1), :].bitcast(I32),
                in_=tab[0, start : start + QUAD * T].rearrange("(r t) -> r t", t=T).bitcast(I32),
            )
        load_w(0, "raw")
        nc.sync.dma_start(out=words[:], in_=tab[0, 0 : 512 * T].rearrange("(p c) -> p c", p=P).bitcast(I32))

        nc.vector.memset(warm[:], 0.0)
        nc.scalar.activation(warm[:], warm[:], GELU)
        nc.gpsimd.memset(b_rows[:], 0.0)
        nc.scalar.dma_start(out=b_rows[0:M_TILES, :], in_=b.rearrange("(m p) -> m p", p=P))
        make_identity(nc, identity[:])
        for r in range(S // RUN):
            for h in range(PASSES):
                nc.gpsimd.memset(scales[r][h][:].bitcast(I32), 0)

        for a in range(PASSES):
            group(nc.scalar.copy, 0, a)
        b_bank = psum.tile([P, N], F32, name="b_bank", tag="acc")
        nc.tensor.transpose(b_bank[:, 0:P], b_rows[:], identity[:])
        nc.scalar.copy(b_cols[:], b_bank[:, 0:M_TILES])

        gather_scales(0)
        load_w(1, "raw")
        quantize(0)
        gather_scales(1)
        load_w(2, "turn0")
        gather_words(0, "words01")
        group(nc.scalar.copy, 1, 0)
        for m in (0, 1):
            product(m, 0)
            store(m, 0, N)
        gather_words(1, "words01")
        for m in (0, 1):
            product(m, 1)
            store(m, N, 2 * N)
        group(nc.vector.tensor_copy, 1, 1)
        quantize(1)
        for m in (2, 3):
            product(m, 0)
            product(m, 1)
            store(m, 0, 2 * N)
        gather_words(2, "turn1")
        for m in range(4):
            product(m, 2)
        gather_words(3, "turn1")
        for m in range(4):
            product(m, 3)
            store(m, 2 * N, 4 * N)
        for i in (2, 3):
            for a in range(PASSES):
                group(nc.vector.tensor_copy, i, a)
            quantize(i)
        for m in range(4, M_TILES):
            product(m, 0)
            product(m, 1)
            store(m, 0, 2 * N)
            product(m, 2)
            if m < M_TILES - 1:
                product(m, 3)
                store(m, 2 * N, 4 * N)
        m, half = M_TILES - 1, N // 2
        store(m, 2 * N, 3 * N)
        product(m, 3, step=half)
        store(m, 3 * N, 3 * N + half)
        store(m, 3 * N + half, 4 * N)
